import numpy as np, ml_dtypes
CORES = [35,38,43,46]
N = 4
import mx_ref
BF = ml_dtypes.bfloat16
def entries(a):
    return np.ascontiguousarray(a.T).reshape(-1)
def table(e):
    return np.ascontiguousarray(np.reshape(e, (-1, 16)).T).astype(np.int32)
def cols(t, e):
    v = np.concatenate([t.reshape(128, -1, 4), np.zeros((128, 1, 4), BF)], axis=1)
    return np.ascontiguousarray(v[:, e]).reshape(128, -1)
def tile(rs):
    return np.stack(rs, axis=2).reshape(128, -1).astype(BF)
def f(rng, *shape):
    return mx_ref.flush((rng.standard_normal(shape, dtype=np.float32) * np.exp2(rng.integers(-2, 3, shape[:-1] + (1,)))).astype(BF))
def wide(rng, *shape, cols=0):
    v = rng.standard_normal(shape, dtype=np.float32) * np.exp2(rng.integers(-12, 13, shape)).astype(np.float32)
    if cols: v *= np.repeat(np.exp2(rng.integers(-cols, cols + 1, shape[:-2] + (1, shape[-1] // 4))) * (rng.random(shape[:-2] + (1, shape[-1] // 4)) > 0.0625), 4, axis=-1).astype(np.float32)
    return mx_ref.flush(v.astype(BF))
T, E, EC, CAPP = 384, 4, 128, 112
def lists(rng, case=""):
    sn, so = np.full((N, N, CAPP), -1), np.full((N, E, EC), -1)
    lone = rng.integers(0, N)
    for d in range(N):
        a = rng.integers(0, E)
        n = rng.integers(CAPP // 4, CAPP + 1, N)
        if case == "full": n[:] = CAPP
        if case == "empty": n[(d + 1) % N] = 0
        if case == "empty" and d == lone: n[np.arange(N) != d] = 0
        used = np.concatenate([s * CAPP + (np.arange(n[s]) if case == "sorted" else rng.permutation(CAPP)[:n[s]]) for s in range(N)])
        if case == "one": used = rng.permutation(N * CAPP)[:EC + rng.integers(E - 1, 8 * E - 7)]
        if case != "sorted": used = rng.permutation(used)
        if case == "empty": used = used[:(E - 1) * EC]
        key = rng.random((E, EC)) * np.exp2(rng.integers(-1, 2, (E, 1)))
        if case in ("full", "one"): key[a] = -1
        if case == "empty": key[a] = 9
        who = np.argsort(key.reshape(-1))[:len(used)] // EC
        if case == "sorted": who = np.sort(who)
        for m in range(E):
            k = used[who == m]; so[d, m, :len(k)] = k
        sn[used // CAPP, d, used % CAPP] = rng.integers(0, T, len(used))
        if case == "sorted":
            for s in range(N): sn[s, d, :n[s]] = np.sort(sn[s, d, :n[s]])
    return {"sn": np.stack([table(q) for q in sn]), "so": np.stack([table(q) for q in so])}
def setup_inputs(rng):
    return {"x": f(rng, N, 128, 4 * T), "w": f(rng, N, 128, 2048 * E), "v": f(rng, N, 128, 512 * E), **lists(rng)}
def setup_inputs_full(rng):
    return {**setup_inputs(rng), **lists(rng, "full")}
def setup_inputs_one(rng):
    return {**setup_inputs(rng), **lists(rng, "one")}
def setup_inputs_empty(rng):
    return {**setup_inputs(rng), **lists(rng, "empty")}
def setup_inputs_sorted(rng):
    return {**setup_inputs(rng), **lists(rng, "sorted")}
def setup_inputs_spread(rng):
    d = setup_inputs(rng); d["x"] = wide(rng, N, 128, 4 * T, cols=6); return d
def check_inputs(d):
    b = []
    for r in range(N):
        c, e = entries(d["sn"][r]), entries(d["so"][r]).reshape(E, EC)
        if c.min() < -1 or c.max() >= T: b.append("sn")
        got = np.concatenate([entries(d["sn"][s])[r * CAPP:(r + 1) * CAPP] for s in range(N)])
        if e.min() < -1 or ((e[:, 1:] >= 0) & (e[:, :-1] < 0)).any() or np.sort(e[e >= 0]).tolist() != np.flatnonzero(got >= 0).tolist(): b.append("so")
    return b
def reference(x, w, v, sn, so):
    y = np.zeros((N, 128, E * EC), np.float32)
    for r in range(N):
        arrived = np.concatenate([cols(x[s], entries(sn[s])[r * CAPP:(r + 1) * CAPP]) for s in range(N)], axis=1)
        e = entries(so[r])
        for m in range(E):
            k = e[EC * m:EC * m + EC]
            t = mx_ref.quantize(cols(arrived, k))
            R = []
            for i in range(4):
                W = mx_ref.quantize(np.ascontiguousarray(w[r][:, 2048 * m + 512 * i:2048 * m + 512 * i + 512]))
                R.append(np.maximum(mx_ref.matmul(W, t), np.float32(0)) * np.float32(0.05))
            z = mx_ref.matmul(mx_ref.quantize(np.ascontiguousarray(v[r][:, 512 * m:512 * m + 512])), mx_ref.quantize(tile(R)))
            y[r][:, EC * m:EC * m + EC] = np.where(k >= 0, z, np.float32(0))
    return {"y": y}

@@ -1,0 +1,249 @@
+from concourse.bass import DstId, RemoteDMATransfer
+from concourse.mybir import AluOpType, ActivationFunctionType, dt
+
+CAPP, TOK, EXP, EC = 112, 384, 4, 128
+Z = 128
+LC = CAPP // 16
+F8 = "float8_e4m3fn_x4"
+
+SCRATCH = {
+    "xb": ("sbuf", [128, 4 * TOK], "bfloat16"),
+    "wb": ("sbuf", [128, 2048 * EXP], "bfloat16"),
+    "vb": ("sbuf", [128, 512 * EXP], "bfloat16"),
+    "zb": ("sbuf", [128, 4 * Z], "bfloat16"),
+    "sn32": ("sbuf", [128, 4 * LC], "int32"),
+    "so32": ("sbuf", [128, EXP * EC // 16], "int32"),
+    "snl": ("sbuf", [128, 64], "uint16"),
+    "sol": ("sbuf", [128, EXP * EC // 16], "uint16"),
+    "xq": ("sbuf", [128, TOK], F8), "xs": ("sbuf", [128, TOK], "uint8"),
+    "wq": ("sbuf", [128, 512 * EXP], F8), "ws": ("sbuf", [128, 512 * EXP], "uint8"),
+    "vq": ("sbuf", [128, 128 * EXP], F8), "vs": ("sbuf", [128, 128 * EXP], "uint8"),
+    "slotq": ("sbuf", [128, 4 * CAPP], F8), "slots": ("sbuf", [128, 4 * CAPP], "uint8"),
+    "landq": ("sbuf", [128, Z + 4 * CAPP], F8), "lands": ("sbuf", [128, Z + 4 * CAPP], "uint8"),
+    "tokq": ("sbuf", [128, EXP * EC], F8), "toks": ("sbuf", [128, EXP * EC], "uint8"),
+    "h": ("sbuf", [128, 4 * EXP * EC], "bfloat16"),
+    "hq": ("sbuf", [128, EXP * EC], F8), "hs": ("sbuf", [128, EXP * EC], "uint8"),
+    "yb": ("sbuf", [128, EXP * EC], "float32"),
+    "ps": ("psum", [128, 4096], "float32"),
+}
+SEMAPHORES = (["ldx", "ldsn", "ldso", "ldw01", "ldw2", "ldw3", "ldv", "zfill", "zquant", "snA", "snB", "sol", "qx",
+               "pqaway", "pqpeer", "pqown", "psaway", "pspeer", "psown", "gate", "sent", "arrq", "arrs", "qv", "ydone"]
+              + ["qw%d" % m for m in range(EXP)] + ["tok%d" % m for m in range(EXP)]
+              + ["mm%d%d" % (m, b) for m in range(EXP) for b in range(4)]
+              + ["relu%d" % m for m in range(EXP)] + ["qh%d" % m for m in range(EXP)]
+              + ["vv%d" % m for m in range(EXP)] + ["yc%d" % m for m in range(EXP)])
+
+
+def routes(src, cores, topo):
+    away = [d for d, c in enumerate(cores) if topo.chip(c) != topo.chip(src)]
+    peer = [d for d, c in enumerate(cores) if topo.chip(c) == topo.chip(src) and c != src]
+    out, used = [], []
+    for i, d in enumerate(away):
+        es = topo.engines(src, cores[d])
+        k = len(es) // len(away)
+        out.append((d, es[i * k:(i + 1) * k]))
+        used += es[i * k:(i + 1) * k]
+    home = [(d, [e for e in topo.engines(src, cores[d]) if e not in used]) for d in peer]
+    return out, home
+
+
+def rank_program(g, core, T, topo):
+    rank = T.rank_of(core)
+    if rank is None:
+        return
+    S = T.sem
+    cores = list(T.cores)
+    ACT = ActivationFunctionType
+    away, home = routes(core, cores, topo)
+    first = away[0][0]
+    na = len(away)
+    peer = home[0][0]
+    arrive = sum(len(es) for c in cores if c != core
+                 for part in routes(c, cores, topo) for d, es in part if d == rank)
+
+    def snoff(d, n):
+        a = d * LC
+        if a % 2:
+            a = 4 * LC + (d - 1) * LC
+        return T.snl[:, a:a + n * LC]
+
+    y = g.sync
+    y.dma_start(T.xb[:], T.x[:]).then_inc(S.ldx, 16)
+    y.dma_start(T.wb[:, 0:4096], T.w[:, 0:4096]).then_inc(S.ldw01, 16)
+    y.wait_ge(S.gate, 1)
+    y.dma_start(T.vb[:], T.v[:]).then_inc(S.ldv, 16)
+    y.dma_start(T.wb[:, 4096:6144], T.w[:, 4096:6144]).then_inc(S.ldw2, 16)
+    y.dma_start(T.wb[:, 6144:8192], T.w[:, 6144:8192]).then_inc(S.ldw3, 16)
+
+    a = g.scalar
+    for k in range(2):
+        a.dma_start(T.sn32[16 * k:16 * k + 16, :], T.sn[:]).then_inc(S.ldsn, 16)
+    for k in range(2):
+        a.dma_start(T.so32[16 * k:16 * k + 16, :], T.so[:]).then_inc(S.ldso, 16)
+
+    v = g.vector
+    v.memset(T.zb[:], 0.0).then_inc(S.zfill, 1)
+    v.wait_ge(S.zfill, 1)
+    v.quantize_mx(T.landq[:, 0:Z], T.lands[:, 0:Z], T.zb[:]).then_inc(S.zquant, 1)
+    v.wait_ge(S.ldsn, 32)
+    for k in range(4):
+        v.tensor_copy(T.snl[32 * k:32 * k + 32, 0:4 * LC], T.sn32[0:32, :]).then_inc(S.snA, 1)
+    for k in range(4):
+        v.tensor_copy(T.snl[32 * k:32 * k + 32, 4 * LC:7 * LC], T.sn32[0:32, LC:4 * LC]).then_inc(S.snB, 1)
+    v.wait_ge(S.ldx, 16)
+    v.quantize_mx(T.xq[:], T.xs[:], T.xb[:]).then_inc(S.qx, 1)
+
+    picks = [("away", "slotq", "slots", 0, na * CAPP, snoff(first, na)),
+             ("peer", "slotq", "slots", na * CAPP, (na + 1) * CAPP, snoff(peer, 1)),
+             ("own", "landq", "lands", Z + rank * CAPP, Z + (rank + 1) * CAPP, snoff(rank, 1))]
+    for eng in (v, a):
+        eng.wait_ge(S.snA, 4)
+        eng.wait_ge(S.qx, 1)
+        for i, (tag, q, s, lo, hi, off) in enumerate(picks):
+            if i == 1:
+                eng.wait_ge(S.snB, 4)
+            if eng is v:
+                v.tensor_copy(T[q][:, lo:hi].bitcast(dt.uint32), T.xq[:, 0:TOK].bitcast(dt.uint32).indirect(off)).then_inc(S["pq" + tag], 1)
+            else:
+                a.activation(T[s][:, lo:hi], T.xs[:, 0:TOK].indirect(off), ACT.Copy).then_inc(S["ps" + tag], 1)
+
+    def send(part, lo, codes):
+        trs = []
+        for i, (d, es) in enumerate(part):
+            rid, pid, _ = topo.addr(cores[d])
+            c0, l0 = (lo + i) * CAPP, Z + rank * CAPP
+            if codes:
+                src, dst = T.slotq[:, c0:c0 + CAPP].bitcast(dt.uint8), T.landq[:, l0:l0 + CAPP].bitcast(dt.uint8)
+            else:
+                src, dst = T.slots[:, c0:c0 + CAPP], T.lands[:, l0:l0 + CAPP]
+            trs.append(RemoteDMATransfer(dst_ids=[DstId(rid=rid, pnc=pid)], dma_engine_mask=sum(1 << e for e in es),
+                                         remote_sem=S.arrq if codes else S.arrs, src=src, dst=dst))
+        g.remote_dma_fused(trs, local_sem=S.sent)
+        return sum(len(es) for _, es in part)
+
+    n = 0
+    g.wait_ge(S.pqaway, 1)
+    n += send(away, 0, True)
+    g.wait_ge(S.psaway, 1)
+    n += send(away, 0, False)
+    g.sem_inc(S.gate, 1)
+    g.wait_ge(S.pqpeer, 1)
+    n += send(home, na, True)
+    g.wait_ge(S.pspeer, 1)
+    n += send(home, na, False)
+    g.wait_ge(S.sent, n)
+
+    v.wait_ge(S.ldso, 32)
+    for k in range(4):
+        v.tensor_scalar(T.sol[32 * k:32 * k + 32, :], T.so32[0:32, :], Z, None, AluOpType.add).then_inc(S.sol, 1)
+
+    def quant_w(m):
+        v.quantize_mx(T.wq[:, 512 * m:512 * m + 512], T.ws[:, 512 * m:512 * m + 512], T.wb[:, 2048 * m:2048 * m + 2048]).then_inc(S["qw%d" % m], 1)
+
+    v.wait_ge(S.ldw01, 16)
+    quant_w(0)
+    quant_w(1)
+
+    def pick(eng, m):
+        lo, hi = EC * m, EC * m + EC
+        off = T.sol[:, EC // 16 * m:EC // 16 * (m + 1)]
+        if eng is v:
+            v.tensor_copy(T.tokq[:, lo:hi].bitcast(dt.uint32), T.landq[:, 0:Z + 4 * CAPP].bitcast(dt.uint32).indirect(off)).then_inc(S["tok%d" % m], 1)
+        else:
+            a.activation(T.toks[:, lo:hi], T.lands[:, 0:Z + 4 * CAPP].indirect(off), ACT.Copy).then_inc(S["tok%d" % m], 1)
+
+    def bank(m, b):
+        k = 512 * (4 * (m % 2) + b)
+        return T.ps[:, k:k + EC]
+
+    def relu(eng, m):
+        for b in ((1, 3) if eng is v else (0, 2)):
+            out = T.h[:, 4 * EC * m + b:4 * EC * (m + 1):4]
+            eng.wait_ge(S["mm%d%d" % (m, b)], 1)
+            if eng is v:
+                v.tensor_scalar(out, bank(m, b), 0.0, 0.05, AluOpType.max, AluOpType.mult).then_inc(S["relu%d" % m], 1)
+            else:
+                a.activation(out, bank(m, b), ACT.Relu, scale=0.05).then_inc(S["relu%d" % m], 1)
+
+    def quant_h(m):
+        v.wait_ge(S["relu%d" % m], 4)
+        v.quantize_mx(T.hq[:, EC * m:EC * m + EC], T.hs[:, EC * m:EC * m + EC], T.h[:, 4 * EC * m:4 * EC * (m + 1)]).then_inc(S["qh%d" % m], 1)
+
+    def copy_y(m):
+        a.wait_ge(S["vv%d" % m], 1)
+        a.activation(T.yb[:, EC * m:EC * m + EC], bank(m, 3), ACT.Copy).then_inc(S["yc%d" % m], 1)
+
+    v.wait_ge(S.zquant, 1)
+    v.wait_ge(S.sol, 4)
+    v.wait_ge(S.pqown, 1)
+    v.wait_ge(S.arrq, arrive)
+    pick(v, 0)
+    pick(v, 1)
+    pick(v, 2)
+    relu(v, 0)
+    pick(v, 3)
+    quant_h(0)
+    v.wait_ge(S.ldv, 16)
+    v.quantize_mx(T.vq[:], T.vs[:], T.vb[:]).then_inc(S.qv, 1)
+    relu(v, 1)
+    quant_h(1)
+    v.wait_ge(S.ldw2, 16)
+    quant_w(2)
+    relu(v, 2)
+    quant_h(2)
+    v.wait_ge(S.ldw3, 16)
+    quant_w(3)
+    relu(v, 3)
+    quant_h(3)
+
+    a.wait_ge(S.zquant, 1)
+    a.wait_ge(S.sol, 4)
+    a.wait_ge(S.psown, 1)
+    a.wait_ge(S.arrs, arrive)
+    pick(a, 0)
+    pick(a, 1)
+    pick(a, 2)
+    relu(a, 0)
+    pick(a, 3)
+    relu(a, 1)
+    copy_y(0)
+    relu(a, 2)
+    copy_y(1)
+    relu(a, 3)
+    copy_y(2)
+    copy_y(3)
+
+    t = g.tensor
+
+    def products_w(m):
+        t.wait_ge(S["qw%d" % m], 1)
+        t.wait_ge(S["tok%d" % m], 2)
+        lo = EC * m
+        for b in range(4):
+            c = 512 * m + 128 * b
+            if b == 3 and m >= 2:
+                t.wait_ge(S["yc%d" % (m - 2)], 1)
+            t.matmul_mx(bank(m, b), T.wq[:, c:c + 128], T.ws[:, c:c + 128], T.tokq[:, lo:lo + EC], T.toks[:, lo:lo + EC],
+                        True, True).then_inc(S["mm%d%d" % (m, b)], 1)
+
+    def product_v(m):
+        t.wait_ge(S["qh%d" % m], 1)
+        if m == 0:
+            t.wait_ge(S.qv, 1)
+        lo = EC * m
+        t.matmul_mx(bank(m, 3), T.vq[:, lo:lo + 128], T.vs[:, lo:lo + 128], T.hq[:, lo:lo + EC], T.hs[:, lo:lo + EC],
+                    True, True).then_inc(S["vv%d" % m], 1)
+
+    products_w(0)
+    products_w(1)
+    product_v(0)
+    products_w(2)
+    product_v(1)
+    products_w(3)
+    product_v(2)
+    product_v(3)
+
+    for m in range(EXP):
+        y.wait_ge(S["yc%d" % m], 1)
+        y.dma_start(T.y[:, EC * m:EC * m + EC], T.yb[:, EC * m:EC * m + EC]).then_inc(S.ydone, 16)
+    y.wait_ge(S.ydone, 16 * EXP)

@@ -6,6 +6,10 @@ Z = 128
 LC = CAPP // 16
 F8 = "float8_e4m3fn_x4"
 
+VECTOR = "w0 w1 v0 w2 P0 P1 P2 P3 R01 R03 w3 Q0 R11 R21 R23 Q1 R31 Q2 R33 Q3 Y2 Y3"
+SCALAR = "S0 S1 S2 S3 R00 R02 R10 R12 R13 R20 R22 R30 R32 Y0 Y1"
+TENSOR = "W0 W1 W2 V0 W3 V1 V2 V3"
+
 SCRATCH = {
     "xb": ("sbuf", [128, 4 * TOK], "bfloat16"),
     "wb": ("sbuf", [128, 2048 * EXP], "bfloat16"),
@@ -27,11 +31,11 @@ SCRATCH = {
     "ps": ("psum", [128, 4096], "float32"),
 }
 SEMAPHORES = (["ldx", "ldsn", "ldso", "ldw01", "ldw2", "ldw3", "ldv", "zfill", "zquant", "snA", "snB", "sol", "qx",
-               "pqaway", "pqpeer", "pqown", "psaway", "pspeer", "psown", "gate", "sent", "arrq", "arrs", "qv", "ydone"]
+               "pqaway", "pqpeer", "pqown", "psaway", "pspeer", "psown", "sent", "arrq", "arrs", "qv", "ydone"]
               + ["qw%d" % m for m in range(EXP)] + ["tok%d" % m for m in range(EXP)]
               + ["mm%d%d" % (m, b) for m in range(EXP) for b in range(4)]
-              + ["relu%d" % m for m in range(EXP)] + ["qh%d" % m for m in range(EXP)]
-              + ["vv%d" % m for m in range(EXP)] + ["yc%d" % m for m in range(EXP)])
+              + ["relu%d%d" % (m, b) for m in range(EXP) for b in range(4)]
+              + ["qh%d" % m for m in range(EXP)] + ["vv%d" % m for m in range(EXP)] + ["yc%d" % m for m in range(EXP)])
 
 
 def routes(src, cores, topo):
@@ -45,6 +49,19 @@ def routes(src, cores, topo):
         used += es[i * k:(i + 1) * k]
     home = [(d, [e for e in topo.engines(src, cores[d]) if e not in used]) for d in peer]
     return out, home
+
+
+def banks():
+    plan, held, i = {}, [None] * 8, 0
+    for t in TENSOR.split():
+        m = int(t[1])
+        for p in ([("W", m, b) for b in range(4)] if t[0] == "W" else [("V", m, 0)]):
+            k = i % 8
+            o = held[k]
+            plan[p] = (k, None if o is None else "relu%d%d" % o[1:] if o[0] == "W" else "yc%d" % o[1])
+            held[k] = p
+            i += 1
+    return plan
 
 
 def rank_program(g, core, T, topo):
@@ -70,7 +87,6 @@ def rank_program(g, core, T, topo):
     y = g.sync
     y.dma_start(T.xb[:], T.x[:]).then_inc(S.ldx, 16)
     y.dma_start(T.wb[:, 0:4096], T.w[:, 0:4096]).then_inc(S.ldw01, 16)
-    y.wait_ge(S.gate, 1)
     y.dma_start(T.vb[:], T.v[:]).then_inc(S.ldv, 16)
     y.dma_start(T.wb[:, 4096:6144], T.w[:, 4096:6144]).then_inc(S.ldw2, 16)
     y.dma_start(T.wb[:, 6144:8192], T.w[:, 6144:8192]).then_inc(S.ldw3, 16)
@@ -126,7 +142,6 @@ def rank_program(g, core, T, topo):
     n += send(away, 0, True)
     g.wait_ge(S.psaway, 1)
     n += send(away, 0, False)
-    g.sem_inc(S.gate, 1)
     g.wait_ge(S.pqpeer, 1)
     n += send(home, na, True)
     g.wait_ge(S.pspeer, 1)
@@ -137,113 +152,85 @@ def rank_program(g, core, T, topo):
     for k in range(4):
         v.tensor_scalar(T.sol[32 * k:32 * k + 32, :], T.so32[0:32, :], Z, None, AluOpType.add).then_inc(S.sol, 1)
 
-    def quant_w(m):
-        v.quantize_mx(T.wq[:, 512 * m:512 * m + 512], T.ws[:, 512 * m:512 * m + 512], T.wb[:, 2048 * m:2048 * m + 2048]).then_inc(S["qw%d" % m], 1)
+    plan = banks()
 
-    v.wait_ge(S.ldw01, 16)
-    quant_w(0)
-    quant_w(1)
+    def bank(p):
+        return T.ps[:, 512 * plan[p][0]:512 * plan[p][0] + EC]
 
-    def pick(eng, m):
-        lo, hi = EC * m, EC * m + EC
-        off = T.sol[:, EC // 16 * m:EC // 16 * (m + 1)]
-        if eng is v:
-            v.tensor_copy(T.tokq[:, lo:hi].bitcast(dt.uint32), T.landq[:, 0:Z + 4 * CAPP].bitcast(dt.uint32).indirect(off)).then_inc(S["tok%d" % m], 1)
-        else:
-            a.activation(T.toks[:, lo:hi], T.lands[:, 0:Z + 4 * CAPP].indirect(off), ACT.Copy).then_inc(S["tok%d" % m], 1)
+    def work(eng, order):
+        vec = eng is v
+        ready = False
+        for step in order.split():
+            k, m = step[0], int(step[1])
+            lo, hi = EC * m, EC * m + EC
+            if k == "w":
+                eng.wait_ge(S.ldw01 if m < 2 else S["ldw%d" % m], 16)
+                v.quantize_mx(T.wq[:, 512 * m:512 * m + 512], T.ws[:, 512 * m:512 * m + 512],
+                              T.wb[:, 2048 * m:2048 * m + 2048]).then_inc(S["qw%d" % m], 1)
+            elif k == "v":
+                eng.wait_ge(S.ldv, 16)
+                v.quantize_mx(T.vq[:], T.vs[:], T.vb[:]).then_inc(S.qv, 1)
+            elif k in "PS":
+                if not ready:
+                    ready = True
+                    eng.wait_ge(S.zquant, 1)
+                    eng.wait_ge(S.sol, 4)
+                    eng.wait_ge(S.pqown if vec else S.psown, 1)
+                    eng.wait_ge(S.arrq if vec else S.arrs, arrive)
+                off = T.sol[:, EC // 16 * m:EC // 16 * (m + 1)]
+                if vec:
+                    v.tensor_copy(T.tokq[:, lo:hi].bitcast(dt.uint32),
+                                  T.landq[:, 0:Z + 4 * CAPP].bitcast(dt.uint32).indirect(off)).then_inc(S["tok%d" % m], 1)
+                else:
+                    a.activation(T.toks[:, lo:hi], T.lands[:, 0:Z + 4 * CAPP].indirect(off), ACT.Copy).then_inc(S["tok%d" % m], 1)
+            elif k == "R":
+                b = int(step[2])
+                out, src, done = T.h[:, 4 * lo + b:4 * hi:4], bank(("W", m, b)), S["relu%d%d" % (m, b)]
+                eng.wait_ge(S["mm%d%d" % (m, b)], 1)
+                if vec:
+                    v.tensor_scalar(out, src, 0.0, 0.05, AluOpType.max, AluOpType.mult).then_inc(done, 1)
+                else:
+                    a.activation(out, src, ACT.Relu, scale=0.05).then_inc(done, 1)
+            elif k == "Q":
+                for b in range(4):
+                    eng.wait_ge(S["relu%d%d" % (m, b)], 1)
+                v.quantize_mx(T.hq[:, lo:hi], T.hs[:, lo:hi], T.h[:, 4 * lo:4 * hi]).then_inc(S["qh%d" % m], 1)
+            elif k == "Y":
+                eng.wait_ge(S["vv%d" % m], 1)
+                if vec:
+                    v.tensor_copy(T.yb[:, lo:hi], bank(("V", m, 0))).then_inc(S["yc%d" % m], 1)
+                else:
+                    a.activation(T.yb[:, lo:hi], bank(("V", m, 0)), ACT.Copy).then_inc(S["yc%d" % m], 1)
 
-    def bank(m, b):
-        k = 512 * (4 * (m % 2) + b)
-        return T.ps[:, k:k + EC]
-
-    def relu(eng, m):
-        for b in ((1, 3) if eng is v else (0, 2)):
-            out = T.h[:, 4 * EC * m + b:4 * EC * (m + 1):4]
-            eng.wait_ge(S["mm%d%d" % (m, b)], 1)
-            if eng is v:
-                v.tensor_scalar(out, bank(m, b), 0.0, 0.05, AluOpType.max, AluOpType.mult).then_inc(S["relu%d" % m], 1)
-            else:
-                a.activation(out, bank(m, b), ACT.Relu, scale=0.05).then_inc(S["relu%d" % m], 1)
-
-    def quant_h(m):
-        v.wait_ge(S["relu%d" % m], 4)
-        v.quantize_mx(T.hq[:, EC * m:EC * m + EC], T.hs[:, EC * m:EC * m + EC], T.h[:, 4 * EC * m:4 * EC * (m + 1)]).then_inc(S["qh%d" % m], 1)
-
-    def copy_y(m):
-        a.wait_ge(S["vv%d" % m], 1)
-        a.activation(T.yb[:, EC * m:EC * m + EC], bank(m, 3), ACT.Copy).then_inc(S["yc%d" % m], 1)
-
-    v.wait_ge(S.zquant, 1)
-    v.wait_ge(S.sol, 4)
-    v.wait_ge(S.pqown, 1)
-    v.wait_ge(S.arrq, arrive)
-    pick(v, 0)
-    pick(v, 1)
-    pick(v, 2)
-    relu(v, 0)
-    pick(v, 3)
-    quant_h(0)
-    v.wait_ge(S.ldv, 16)
-    v.quantize_mx(T.vq[:], T.vs[:], T.vb[:]).then_inc(S.qv, 1)
-    relu(v, 1)
-    quant_h(1)
-    v.wait_ge(S.ldw2, 16)
-    quant_w(2)
-    relu(v, 2)
-    quant_h(2)
-    v.wait_ge(S.ldw3, 16)
-    quant_w(3)
-    relu(v, 3)
-    quant_h(3)
-
-    a.wait_ge(S.zquant, 1)
-    a.wait_ge(S.sol, 4)
-    a.wait_ge(S.psown, 1)
-    a.wait_ge(S.arrs, arrive)
-    pick(a, 0)
-    pick(a, 1)
-    pick(a, 2)
-    relu(a, 0)
-    pick(a, 3)
-    relu(a, 1)
-    copy_y(0)
-    relu(a, 2)
-    copy_y(1)
-    relu(a, 3)
-    copy_y(2)
-    copy_y(3)
+    work(v, VECTOR)
+    work(a, SCALAR)
 
     t = g.tensor
+    qv_seen = False
+    for step in TENSOR.split():
+        m = int(step[1])
+        lo, hi = EC * m, EC * m + EC
+        if step[0] == "W":
+            t.wait_ge(S["qw%d" % m], 1)
+            t.wait_ge(S["tok%d" % m], 2)
+            for b in range(4):
+                c = 512 * m + 128 * b
+                if plan[("W", m, b)][1]:
+                    t.wait_ge(S[plan[("W", m, b)][1]], 1)
+                t.matmul_mx(bank(("W", m, b)), T.wq[:, c:c + 128], T.ws[:, c:c + 128], T.tokq[:, lo:hi], T.toks[:, lo:hi],
+                            True, True).then_inc(S["mm%d%d" % (m, b)], 1)
+        else:
+            if not qv_seen:
+                qv_seen = True
+                t.wait_ge(S.qv, 1)
+            t.wait_ge(S["qh%d" % m], 1)
+            if plan[("V", m, 0)][1]:
+                t.wait_ge(S[plan[("V", m, 0)][1]], 1)
+            t.matmul_mx(bank(("V", m, 0)), T.vq[:, lo:lo + 128], T.vs[:, lo:lo + 128], T.hq[:, lo:hi], T.hs[:, lo:hi],
+                        True, True).then_inc(S["vv%d" % m], 1)
 
-    def products_w(m):
-        t.wait_ge(S["qw%d" % m], 1)
-        t.wait_ge(S["tok%d" % m], 2)
-        lo = EC * m
-        for b in range(4):
-            c = 512 * m + 128 * b
-            if b == 3 and m >= 2:
-                t.wait_ge(S["yc%d" % (m - 2)], 1)
-            t.matmul_mx(bank(m, b), T.wq[:, c:c + 128], T.ws[:, c:c + 128], T.tokq[:, lo:lo + EC], T.toks[:, lo:lo + EC],
-                        True, True).then_inc(S["mm%d%d" % (m, b)], 1)
-
-    def product_v(m):
-        t.wait_ge(S["qh%d" % m], 1)
-        if m == 0:
-            t.wait_ge(S.qv, 1)
-        lo = EC * m
-        t.matmul_mx(bank(m, 3), T.vq[:, lo:lo + 128], T.vs[:, lo:lo + 128], T.hq[:, lo:lo + EC], T.hs[:, lo:lo + EC],
-                    True, True).then_inc(S["vv%d" % m], 1)
-
-    products_w(0)
-    products_w(1)
-    product_v(0)
-    products_w(2)
-    product_v(1)
-    products_w(3)
-    product_v(2)
-    product_v(3)
-
-    for m in range(EXP):
+    for m in range(0, EXP, 2):
         y.wait_ge(S["yc%d" % m], 1)
-        y.dma_start(T.y[:, EC * m:EC * m + EC], T.yb[:, EC * m:EC * m + EC]).then_inc(S.ydone, 16)
-    y.wait_ge(S.ydone, 16 * EXP)
+        y.wait_ge(S["yc%d" % (m + 1)], 1)
+        y.dma_start(T.y[:, EC * m:EC * m + 2 * EC], T.yb[:, EC * m:EC * m + 2 * EC]).then_inc(S.ydone, 16)
+    y.wait_ge(S.ydone, 8 * EXP)

@@ -6,9 +6,13 @@ Z = 128
 LC = CAPP // 16
 F8 = "float8_e4m3fn_x4"
 
-VECTOR = "w0 w1 v0 w2 P0 P1 P2 P3 R01 R03 w3 Q0 R11 R21 R23 Q1 R31 Q2 R33 Q3 Y2 Y3"
-SCALAR = "S0 S1 S2 S3 R00 R02 R10 R12 R13 R20 R22 R30 R32 Y0 Y1"
-TENSOR = "W0 W1 W2 V0 W3 V1 V2 V3"
+LOADS = "x n w02 w23 ?aq w34 v04"
+SENDS = "aq as pq ps"
+VECTOR = "z n x a N p o w0 w1 l w2 P0 P1 P2 P3 R01 R03 w3 R11 Q0 R21 v04 R23 Q1 R31 Q2 R33 Q3 Y2 Y3"
+SCALAR = "a p o S0 S1 S2 S3 R00 R02 R10 R12 R13 R20 R22 R30 R32 Y0 Y1"
+TENSOR = "W0 W1 W2 W3 V0 V1 V2 V3"
+STORES = "02 23 34"
+PEER = 8
 
 SCRATCH = {
     "xb": ("sbuf", [128, 4 * TOK], "bfloat16"),
@@ -30,12 +34,10 @@ SCRATCH = {
     "yb": ("sbuf", [128, EXP * EC], "float32"),
     "ps": ("psum", [128, 4096], "float32"),
 }
-SEMAPHORES = (["ldx", "ldsn", "ldso", "ldw01", "ldw2", "ldw3", "ldv", "zfill", "zquant", "snA", "snB", "sol", "qx",
-               "pqaway", "pqpeer", "pqown", "psaway", "pspeer", "psown", "sent", "arrq", "arrs", "qv", "ydone"]
-              + ["qw%d" % m for m in range(EXP)] + ["tok%d" % m for m in range(EXP)]
-              + ["mm%d%d" % (m, b) for m in range(EXP) for b in range(4)]
-              + ["relu%d%d" % (m, b) for m in range(EXP) for b in range(4)]
-              + ["qh%d" % m for m in range(EXP)] + ["vv%d" % m for m in range(EXP)] + ["yc%d" % m for m in range(EXP)])
+SEMAPHORES = (["ldx", "ldsn", "ldso", "zfill", "zquant", "snA", "snB", "sol", "qx", "pqa", "pqp", "pqo", "psa", "psp", "pso",
+               "sentaq", "sentas", "sentpq", "sentps", "arrq", "arrs", "ydone"]
+              + [k + "%d" % m for k in ("ldw", "ldv", "qw", "qv", "tok", "qh", "vv", "yc") for m in range(EXP)]
+              + [k + "%d%d" % (m, b) for k in ("mm", "relu") for m in range(EXP) for b in range(4)])
 
 
 def routes(src, cores, topo):
@@ -47,7 +49,10 @@ def routes(src, cores, topo):
         k = len(es) // len(away)
         out.append((d, es[i * k:(i + 1) * k]))
         used += es[i * k:(i + 1) * k]
-    home = [(d, [e for e in topo.engines(src, cores[d]) if e not in used]) for d in peer]
+    home = []
+    for d in peer:
+        es = [e for e in topo.engines(src, cores[d]) if e not in used]
+        home.append((d, es[::len(es) // PEER]))
     return out, home
 
 
@@ -77,105 +82,127 @@ def rank_program(g, core, T, topo):
     peer = home[0][0]
     arrive = sum(len(es) for c in cores if c != core
                  for part in routes(c, cores, topo) for d, es in part if d == rank)
-
-    def snoff(d, n):
-        a = d * LC
-        if a % 2:
-            a = 4 * LC + (d - 1) * LC
-        return T.snl[:, a:a + n * LC]
-
-    y = g.sync
-    y.dma_start(T.xb[:], T.x[:]).then_inc(S.ldx, 16)
-    y.dma_start(T.wb[:, 0:4096], T.w[:, 0:4096]).then_inc(S.ldw01, 16)
-    y.dma_start(T.vb[:], T.v[:]).then_inc(S.ldv, 16)
-    y.dma_start(T.wb[:, 4096:6144], T.w[:, 4096:6144]).then_inc(S.ldw2, 16)
-    y.dma_start(T.wb[:, 6144:8192], T.w[:, 6144:8192]).then_inc(S.ldw3, 16)
+    nsent = {"a": sum(len(es) for _, es in away), "p": sum(len(es) for _, es in home)}
+    tk = lambda s: s.split()
 
     a = g.scalar
-    for k in range(2):
-        a.dma_start(T.sn32[16 * k:16 * k + 16, :], T.sn[:]).then_inc(S.ldsn, 16)
+    a.dma_start(T.sn32[0:16, :], T.sn[:]).then_inc(S.ldsn, 16)
     for k in range(2):
         a.dma_start(T.so32[16 * k:16 * k + 16, :], T.so[:]).then_inc(S.ldso, 16)
 
-    v = g.vector
-    v.memset(T.zb[:], 0.0).then_inc(S.zfill, 1)
-    v.wait_ge(S.zfill, 1)
-    v.quantize_mx(T.landq[:, 0:Z], T.lands[:, 0:Z], T.zb[:]).then_inc(S.zquant, 1)
-    v.wait_ge(S.ldsn, 32)
-    for k in range(4):
-        v.tensor_copy(T.snl[32 * k:32 * k + 32, 0:4 * LC], T.sn32[0:32, :]).then_inc(S.snA, 1)
-    for k in range(4):
-        v.tensor_copy(T.snl[32 * k:32 * k + 32, 4 * LC:7 * LC], T.sn32[0:32, LC:4 * LC]).then_inc(S.snB, 1)
-    v.wait_ge(S.ldx, 16)
-    v.quantize_mx(T.xq[:], T.xs[:], T.xb[:]).then_inc(S.qx, 1)
+    y = g.sync
+    ldof = {}
+    for s in tk(LOADS):
+        if s == "x":
+            y.dma_start(T.xb[:], T.x[:]).then_inc(S.ldx, 16)
+        elif s == "n":
+            y.dma_start(T.sn32[16:32, :], T.sn[:]).then_inc(S.ldsn, 16)
+        elif s[0] == "?":
+            y.wait_ge(S["sent" + s[1:]], nsent[s[1]])
+        else:
+            lo, hi = int(s[1]), int(s[2])
+            n, dst, src = (2048, T.wb, T.w) if s[0] == "w" else (512, T.vb, T.v)
+            for m in range(lo, hi):
+                ldof[s[0], m] = "ld%s%d" % (s[0], lo)
+            y.dma_start(dst[:, n * lo:n * hi], src[:, n * lo:n * hi]).then_inc(S["ld%s%d" % (s[0], lo)], 16)
 
-    picks = [("away", "slotq", "slots", 0, na * CAPP, snoff(first, na)),
-             ("peer", "slotq", "slots", na * CAPP, (na + 1) * CAPP, snoff(peer, 1)),
-             ("own", "landq", "lands", Z + rank * CAPP, Z + (rank + 1) * CAPP, snoff(rank, 1))]
-    for eng in (v, a):
-        eng.wait_ge(S.snA, 4)
-        eng.wait_ge(S.qx, 1)
-        for i, (tag, q, s, lo, hi, off) in enumerate(picks):
-            if i == 1:
-                eng.wait_ge(S.snB, 4)
-            if eng is v:
-                v.tensor_copy(T[q][:, lo:hi].bitcast(dt.uint32), T.xq[:, 0:TOK].bitcast(dt.uint32).indirect(off)).then_inc(S["pq" + tag], 1)
-            else:
-                a.activation(T[s][:, lo:hi], T.xs[:, 0:TOK].indirect(off), ACT.Copy).then_inc(S["ps" + tag], 1)
+    def snoff(d, n):
+        c = d * LC
+        if c % 2:
+            c = 4 * LC + (d - 1) * LC
+        return T.snl[:, c:c + n * LC]
 
-    def send(part, lo, codes):
+    picks = {"a": ("slotq", "slots", 0, na * CAPP, snoff(first, na)),
+             "p": ("slotq", "slots", na * CAPP, (na + 1) * CAPP, snoff(peer, 1)),
+             "o": ("landq", "lands", Z + rank * CAPP, Z + (rank + 1) * CAPP, snoff(rank, 1))}
+
+    for s in tk(SENDS):
+        part, lo = (away, 0) if s[0] == "a" else (home, na)
         trs = []
         for i, (d, es) in enumerate(part):
             rid, pid, _ = topo.addr(cores[d])
             c0, l0 = (lo + i) * CAPP, Z + rank * CAPP
-            if codes:
+            if s[1] == "q":
                 src, dst = T.slotq[:, c0:c0 + CAPP].bitcast(dt.uint8), T.landq[:, l0:l0 + CAPP].bitcast(dt.uint8)
             else:
                 src, dst = T.slots[:, c0:c0 + CAPP], T.lands[:, l0:l0 + CAPP]
             trs.append(RemoteDMATransfer(dst_ids=[DstId(rid=rid, pnc=pid)], dma_engine_mask=sum(1 << e for e in es),
-                                         remote_sem=S.arrq if codes else S.arrs, src=src, dst=dst))
-        g.remote_dma_fused(trs, local_sem=S.sent)
-        return sum(len(es) for _, es in part)
-
-    n = 0
-    g.wait_ge(S.pqaway, 1)
-    n += send(away, 0, True)
-    g.wait_ge(S.psaway, 1)
-    n += send(away, 0, False)
-    g.wait_ge(S.pqpeer, 1)
-    n += send(home, na, True)
-    g.wait_ge(S.pspeer, 1)
-    n += send(home, na, False)
-    g.wait_ge(S.sent, n)
-
-    v.wait_ge(S.ldso, 32)
-    for k in range(4):
-        v.tensor_scalar(T.sol[32 * k:32 * k + 32, :], T.so32[0:32, :], Z, None, AluOpType.add).then_inc(S.sol, 1)
+                                         remote_sem=S.arrq if s[1] == "q" else S.arrs, src=src, dst=dst))
+        g.wait_ge(S["p%s%s" % (s[1], s[0])], 1)
+        g.remote_dma_fused(trs, local_sem=S["sent" + s])
+    for s in tk(SENDS):
+        g.wait_ge(S["sent" + s], nsent[s[0]])
 
     plan = banks()
+    v = g.vector
+    qvof = {}
+    for s in tk(VECTOR):
+        if s[0] == "v":
+            for m in range(int(s[1]), int(s[2])):
+                qvof[m] = "qv" + s[1]
 
     def bank(p):
         return T.ps[:, 512 * plan[p][0]:512 * plan[p][0] + EC]
 
     def work(eng, order):
         vec = eng is v
-        ready = False
-        for step in order.split():
-            k, m = step[0], int(step[1])
+        seen = []
+        for step in tk(order):
+            k = step[0]
+            if k == "z":
+                v.memset(T.zb[:], 0.0).then_inc(S.zfill, 1)
+                v.wait_ge(S.zfill, 1)
+                v.quantize_mx(T.landq[:, 0:Z], T.lands[:, 0:Z], T.zb[:]).then_inc(S.zquant, 1)
+                continue
+            if k == "n":
+                v.wait_ge(S.ldsn, 32)
+                for j in range(4):
+                    v.tensor_copy(T.snl[32 * j:32 * j + 32, 0:4 * LC], T.sn32[0:32, :]).then_inc(S.snA, 1)
+                continue
+            if k == "N":
+                for j in range(4):
+                    v.tensor_copy(T.snl[32 * j:32 * j + 32, 4 * LC:7 * LC], T.sn32[0:32, LC:4 * LC]).then_inc(S.snB, 1)
+                continue
+            if k == "l":
+                v.wait_ge(S.ldso, 32)
+                for j in range(4):
+                    v.tensor_scalar(T.sol[32 * j:32 * j + 32, :], T.so32[0:32, :], Z, None, AluOpType.add).then_inc(S.sol, 1)
+                continue
+            if k == "x":
+                v.wait_ge(S.ldx, 16)
+                v.quantize_mx(T.xq[:], T.xs[:], T.xb[:]).then_inc(S.qx, 1)
+                continue
+            if k in "apo":
+                if "x" not in seen:
+                    seen.append("x")
+                    eng.wait_ge(S.snA, 4)
+                    eng.wait_ge(S.qx, 1)
+                if k != "a" and "N" not in seen:
+                    seen.append("N")
+                    eng.wait_ge(S.snB, 4)
+                q, s, lo, hi, off = picks[k]
+                if vec:
+                    v.tensor_copy(T[q][:, lo:hi].bitcast(dt.uint32), T.xq[:, 0:TOK].bitcast(dt.uint32).indirect(off)).then_inc(S["pq" + k], 1)
+                else:
+                    a.activation(T[s][:, lo:hi], T.xs[:, 0:TOK].indirect(off), ACT.Copy).then_inc(S["ps" + k], 1)
+                continue
+            m = int(step[1])
             lo, hi = EC * m, EC * m + EC
             if k == "w":
-                eng.wait_ge(S.ldw01 if m < 2 else S["ldw%d" % m], 16)
+                eng.wait_ge(S[ldof["w", m]], 16)
                 v.quantize_mx(T.wq[:, 512 * m:512 * m + 512], T.ws[:, 512 * m:512 * m + 512],
                               T.wb[:, 2048 * m:2048 * m + 2048]).then_inc(S["qw%d" % m], 1)
             elif k == "v":
-                eng.wait_ge(S.ldv, 16)
-                v.quantize_mx(T.vq[:], T.vs[:], T.vb[:]).then_inc(S.qv, 1)
+                hi = EC * int(step[2])
+                for sm in sorted({ldof["v", j] for j in range(m, int(step[2]))}):
+                    eng.wait_ge(S[sm], 16)
+                v.quantize_mx(T.vq[:, lo:hi], T.vs[:, lo:hi], T.vb[:, 4 * lo:4 * hi]).then_inc(S["qv%d" % m], 1)
             elif k in "PS":
-                if not ready:
-                    ready = True
+                if "w" not in seen:
+                    seen.append("w")
                     eng.wait_ge(S.zquant, 1)
                     eng.wait_ge(S.sol, 4)
-                    eng.wait_ge(S.pqown if vec else S.psown, 1)
+                    eng.wait_ge(S.pqo if vec else S.pso, 1)
                     eng.wait_ge(S.arrq if vec else S.arrs, arrive)
                 off = T.sol[:, EC // 16 * m:EC // 16 * (m + 1)]
                 if vec:
@@ -206,8 +233,8 @@ def rank_program(g, core, T, topo):
     work(a, SCALAR)
 
     t = g.tensor
-    qv_seen = False
-    for step in TENSOR.split():
+    seen = []
+    for step in tk(TENSOR):
         m = int(step[1])
         lo, hi = EC * m, EC * m + EC
         if step[0] == "W":
@@ -220,17 +247,20 @@ def rank_program(g, core, T, topo):
                 t.matmul_mx(bank(("W", m, b)), T.wq[:, c:c + 128], T.ws[:, c:c + 128], T.tokq[:, lo:hi], T.toks[:, lo:hi],
                             True, True).then_inc(S["mm%d%d" % (m, b)], 1)
         else:
-            if not qv_seen:
-                qv_seen = True
-                t.wait_ge(S.qv, 1)
+            if qvof[m] not in seen:
+                seen.append(qvof[m])
+                t.wait_ge(S[qvof[m]], 1)
             t.wait_ge(S["qh%d" % m], 1)
             if plan[("V", m, 0)][1]:
                 t.wait_ge(S[plan[("V", m, 0)][1]], 1)
             t.matmul_mx(bank(("V", m, 0)), T.vq[:, lo:lo + 128], T.vs[:, lo:lo + 128], T.hq[:, lo:hi], T.hs[:, lo:hi],
                         True, True).then_inc(S["vv%d" % m], 1)
 
-    for m in range(0, EXP, 2):
-        y.wait_ge(S["yc%d" % m], 1)
-        y.wait_ge(S["yc%d" % (m + 1)], 1)
-        y.dma_start(T.y[:, EC * m:EC * m + 2 * EC], T.yb[:, EC * m:EC * m + 2 * EC]).then_inc(S.ydone, 16)
-    y.wait_ge(S.ydone, 8 * EXP)
+    k = 0
+    for s in tk(STORES):
+        lo, hi = int(s[0]), int(s[1])
+        for m in range(lo, hi):
+            y.wait_ge(S["yc%d" % m], 1)
+        y.dma_start(T.y[:, EC * lo:EC * hi], T.yb[:, EC * lo:EC * hi]).then_inc(S.ydone, 16)
+        k += 16
+    y.wait_ge(S.ydone, k)

from concourse.bass import DstId, RemoteDMATransfer
from concourse.mybir import AluOpType, ActivationFunctionType, dt

CAPP, TOK, EXP, EC = 112, 384, 4, 128
Z = 128
LC = CAPP // 16
F8 = "float8_e4m3fn_x4"

LOADS = "x n w02 w23 ?aq w34 v04"
SENDS = "aq as pq ps"
VECTOR = "z n x a N p o w0 w1 l w2 P0 P1 P2 P3 R01 R03 w3 R11 Q0 R21 v04 R23 Q1 R31 Q2 R33 Q3 Y2 Y3"
SCALAR = "a p o S0 S1 S2 S3 R00 R02 R10 R12 R13 R20 R22 R30 R32 Y0 Y1"
TENSOR = "W0 W1 W2 W3 V0 V1 V2 V3"
STORES = "02 23 34"
PEER = 8

SCRATCH = {
    "xb": ("sbuf", [128, 4 * TOK], "bfloat16"),
    "wb": ("sbuf", [128, 2048 * EXP], "bfloat16"),
    "vb": ("sbuf", [128, 512 * EXP], "bfloat16"),
    "zb": ("sbuf", [128, 4 * Z], "bfloat16"),
    "sn32": ("sbuf", [128, 4 * LC], "int32"),
    "so32": ("sbuf", [128, EXP * EC // 16], "int32"),
    "snl": ("sbuf", [128, 64], "uint16"),
    "sol": ("sbuf", [128, EXP * EC // 16], "uint16"),
    "xq": ("sbuf", [128, TOK], F8), "xs": ("sbuf", [128, TOK], "uint8"),
    "wq": ("sbuf", [128, 512 * EXP], F8), "ws": ("sbuf", [128, 512 * EXP], "uint8"),
    "vq": ("sbuf", [128, 128 * EXP], F8), "vs": ("sbuf", [128, 128 * EXP], "uint8"),
    "slotq": ("sbuf", [128, 4 * CAPP], F8), "slots": ("sbuf", [128, 4 * CAPP], "uint8"),
    "landq": ("sbuf", [128, Z + 4 * CAPP], F8), "lands": ("sbuf", [128, Z + 4 * CAPP], "uint8"),
    "tokq": ("sbuf", [128, EXP * EC], F8), "toks": ("sbuf", [128, EXP * EC], "uint8"),
    "h": ("sbuf", [128, 4 * EXP * EC], "bfloat16"),
    "hq": ("sbuf", [128, EXP * EC], F8), "hs": ("sbuf", [128, EXP * EC], "uint8"),
    "yb": ("sbuf", [128, EXP * EC], "float32"),
    "ps": ("psum", [128, 4096], "float32"),
}
SEMAPHORES = (["ldx", "ldsn", "ldso", "zfill", "zquant", "snA", "snB", "sol", "qx", "pqa", "pqp", "pqo", "psa", "psp", "pso",
               "sentaq", "sentas", "sentpq", "sentps", "arrq", "arrs", "ydone"]
              + [k + "%d" % m for k in ("ldw", "ldv", "qw", "qv", "tok", "qh", "vv", "yc") for m in range(EXP)]
              + [k + "%d%d" % (m, b) for k in ("mm", "relu") for m in range(EXP) for b in range(4)])


def routes(src, cores, topo):
    away = [d for d, c in enumerate(cores) if topo.chip(c) != topo.chip(src)]
    peer = [d for d, c in enumerate(cores) if topo.chip(c) == topo.chip(src) and c != src]
    out, used = [], []
    for i, d in enumerate(away):
        es = topo.engines(src, cores[d])
        k = len(es) // len(away)
        out.append((d, es[i * k:(i + 1) * k]))
        used += es[i * k:(i + 1) * k]
    home = []
    for d in peer:
        es = [e for e in topo.engines(src, cores[d]) if e not in used]
        home.append((d, es[::len(es) // PEER]))
    return out, home


def banks():
    plan, held, i = {}, [None] * 8, 0
    for t in TENSOR.split():
        m = int(t[1])
        for p in ([("W", m, b) for b in range(4)] if t[0] == "W" else [("V", m, 0)]):
            k = i % 8
            o = held[k]
            plan[p] = (k, None if o is None else "relu%d%d" % o[1:] if o[0] == "W" else "yc%d" % o[1])
            held[k] = p
            i += 1
    return plan


def rank_program(g, core, T, topo):
    rank = T.rank_of(core)
    if rank is None:
        return
    S = T.sem
    cores = list(T.cores)
    ACT = ActivationFunctionType
    away, home = routes(core, cores, topo)
    first = away[0][0]
    na = len(away)
    peer = home[0][0]
    arrive = sum(len(es) for c in cores if c != core
                 for part in routes(c, cores, topo) for d, es in part if d == rank)
    nsent = {"a": sum(len(es) for _, es in away), "p": sum(len(es) for _, es in home)}
    tk = lambda s: s.split()

    a = g.scalar
    a.dma_start(T.sn32[0:16, :], T.sn[:]).then_inc(S.ldsn, 16)
    for k in range(2):
        a.dma_start(T.so32[16 * k:16 * k + 16, :], T.so[:]).then_inc(S.ldso, 16)

    y = g.sync
    ldof = {}
    for s in tk(LOADS):
        if s == "x":
            y.dma_start(T.xb[:], T.x[:]).then_inc(S.ldx, 16)
        elif s == "n":
            y.dma_start(T.sn32[16:32, :], T.sn[:]).then_inc(S.ldsn, 16)
        elif s[0] == "?":
            y.wait_ge(S["sent" + s[1:]], nsent[s[1]])
        else:
            lo, hi = int(s[1]), int(s[2])
            n, dst, src = (2048, T.wb, T.w) if s[0] == "w" else (512, T.vb, T.v)
            for m in range(lo, hi):
                ldof[s[0], m] = "ld%s%d" % (s[0], lo)
            y.dma_start(dst[:, n * lo:n * hi], src[:, n * lo:n * hi]).then_inc(S["ld%s%d" % (s[0], lo)], 16)

    def snoff(d, n):
        c = d * LC
        if c % 2:
            c = 4 * LC + (d - 1) * LC
        return T.snl[:, c:c + n * LC]

    picks = {"a": ("slotq", "slots", 0, na * CAPP, snoff(first, na)),
             "p": ("slotq", "slots", na * CAPP, (na + 1) * CAPP, snoff(peer, 1)),
             "o": ("landq", "lands", Z + rank * CAPP, Z + (rank + 1) * CAPP, snoff(rank, 1))}

    for s in tk(SENDS):
        part, lo = (away, 0) if s[0] == "a" else (home, na)
        trs = []
        for i, (d, es) in enumerate(part):
            rid, pid, _ = topo.addr(cores[d])
            c0, l0 = (lo + i) * CAPP, Z + rank * CAPP
            if s[1] == "q":
                src, dst = T.slotq[:, c0:c0 + CAPP].bitcast(dt.uint8), T.landq[:, l0:l0 + CAPP].bitcast(dt.uint8)
            else:
                src, dst = T.slots[:, c0:c0 + CAPP], T.lands[:, l0:l0 + CAPP]
            trs.append(RemoteDMATransfer(dst_ids=[DstId(rid=rid, pnc=pid)], dma_engine_mask=sum(1 << e for e in es),
                                         remote_sem=S.arrq if s[1] == "q" else S.arrs, src=src, dst=dst))
        g.wait_ge(S["p%s%s" % (s[1], s[0])], 1)
        g.remote_dma_fused(trs, local_sem=S["sent" + s])
    for s in tk(SENDS):
        g.wait_ge(S["sent" + s], nsent[s[0]])

    plan = banks()
    v = g.vector
    qvof = {}
    for s in tk(VECTOR):
        if s[0] == "v":
            for m in range(int(s[1]), int(s[2])):
                qvof[m] = "qv" + s[1]

    def bank(p):
        return T.ps[:, 512 * plan[p][0]:512 * plan[p][0] + EC]

    def work(eng, order):
        vec = eng is v
        seen = []
        for step in tk(order):
            k = step[0]
            if k == "z":
                v.memset(T.zb[:], 0.0).then_inc(S.zfill, 1)
                v.wait_ge(S.zfill, 1)
                v.quantize_mx(T.landq[:, 0:Z], T.lands[:, 0:Z], T.zb[:]).then_inc(S.zquant, 1)
                continue
            if k == "n":
                v.wait_ge(S.ldsn, 32)
                for j in range(4):
                    v.tensor_copy(T.snl[32 * j:32 * j + 32, 0:4 * LC], T.sn32[0:32, :]).then_inc(S.snA, 1)
                continue
            if k == "N":
                for j in range(4):
                    v.tensor_copy(T.snl[32 * j:32 * j + 32, 4 * LC:7 * LC], T.sn32[0:32, LC:4 * LC]).then_inc(S.snB, 1)
                continue
            if k == "l":
                v.wait_ge(S.ldso, 32)
                for j in range(4):
                    v.tensor_scalar(T.sol[32 * j:32 * j + 32, :], T.so32[0:32, :], Z, None, AluOpType.add).then_inc(S.sol, 1)
                continue
            if k == "x":
                v.wait_ge(S.ldx, 16)
                v.quantize_mx(T.xq[:], T.xs[:], T.xb[:]).then_inc(S.qx, 1)
                continue
            if k in "apo":
                if "x" not in seen:
                    seen.append("x")
                    eng.wait_ge(S.snA, 4)
                    eng.wait_ge(S.qx, 1)
                if k != "a" and "N" not in seen:
                    seen.append("N")
                    eng.wait_ge(S.snB, 4)
                q, s, lo, hi, off = picks[k]
                if vec:
                    v.tensor_copy(T[q][:, lo:hi].bitcast(dt.uint32), T.xq[:, 0:TOK].bitcast(dt.uint32).indirect(off)).then_inc(S["pq" + k], 1)
                else:
                    a.activation(T[s][:, lo:hi], T.xs[:, 0:TOK].indirect(off), ACT.Copy).then_inc(S["ps" + k], 1)
                continue
            m = int(step[1])
            lo, hi = EC * m, EC * m + EC
            if k == "w":
                eng.wait_ge(S[ldof["w", m]], 16)
                v.quantize_mx(T.wq[:, 512 * m:512 * m + 512], T.ws[:, 512 * m:512 * m + 512],
                              T.wb[:, 2048 * m:2048 * m + 2048]).then_inc(S["qw%d" % m], 1)
            elif k == "v":
                hi = EC * int(step[2])
                for sm in sorted({ldof["v", j] for j in range(m, int(step[2]))}):
                    eng.wait_ge(S[sm], 16)
                v.quantize_mx(T.vq[:, lo:hi], T.vs[:, lo:hi], T.vb[:, 4 * lo:4 * hi]).then_inc(S["qv%d" % m], 1)
            elif k in "PS":
                if "w" not in seen:
                    seen.append("w")
                    eng.wait_ge(S.zquant, 1)
                    eng.wait_ge(S.sol, 4)
                    eng.wait_ge(S.pqo if vec else S.pso, 1)
                    eng.wait_ge(S.arrq if vec else S.arrs, arrive)
                off = T.sol[:, EC // 16 * m:EC // 16 * (m + 1)]
                if vec:
                    v.tensor_copy(T.tokq[:, lo:hi].bitcast(dt.uint32),
                                  T.landq[:, 0:Z + 4 * CAPP].bitcast(dt.uint32).indirect(off)).then_inc(S["tok%d" % m], 1)
                else:
                    a.activation(T.toks[:, lo:hi], T.lands[:, 0:Z + 4 * CAPP].indirect(off), ACT.Copy).then_inc(S["tok%d" % m], 1)
            elif k == "R":
                b = int(step[2])
                out, src, done = T.h[:, 4 * lo + b:4 * hi:4], bank(("W", m, b)), S["relu%d%d" % (m, b)]
                eng.wait_ge(S["mm%d%d" % (m, b)], 1)
                if vec:
                    v.tensor_scalar(out, src, 0.0, 0.05, AluOpType.max, AluOpType.mult).then_inc(done, 1)
                else:
                    a.activation(out, src, ACT.Relu, scale=0.05).then_inc(done, 1)
            elif k == "Q":
                for b in range(4):
                    eng.wait_ge(S["relu%d%d" % (m, b)], 1)
                v.quantize_mx(T.hq[:, lo:hi], T.hs[:, lo:hi], T.h[:, 4 * lo:4 * hi]).then_inc(S["qh%d" % m], 1)
            elif k == "Y":
                eng.wait_ge(S["vv%d" % m], 1)
                if vec:
                    v.tensor_copy(T.yb[:, lo:hi], bank(("V", m, 0))).then_inc(S["yc%d" % m], 1)
                else:
                    a.activation(T.yb[:, lo:hi], bank(("V", m, 0)), ACT.Copy).then_inc(S["yc%d" % m], 1)

    work(v, VECTOR)
    work(a, SCALAR)

    t = g.tensor
    seen = []
    for step in tk(TENSOR):
        m = int(step[1])
        lo, hi = EC * m, EC * m + EC
        if step[0] == "W":
            t.wait_ge(S["qw%d" % m], 1)
            t.wait_ge(S["tok%d" % m], 2)
            for b in range(4):
                c = 512 * m + 128 * b
                if plan[("W", m, b)][1]:
                    t.wait_ge(S[plan[("W", m, b)][1]], 1)
                t.matmul_mx(bank(("W", m, b)), T.wq[:, c:c + 128], T.ws[:, c:c + 128], T.tokq[:, lo:hi], T.toks[:, lo:hi],
                            True, True).then_inc(S["mm%d%d" % (m, b)], 1)
        else:
            if qvof[m] not in seen:
                seen.append(qvof[m])
                t.wait_ge(S[qvof[m]], 1)
            t.wait_ge(S["qh%d" % m], 1)
            if plan[("V", m, 0)][1]:
                t.wait_ge(S[plan[("V", m, 0)][1]], 1)
            t.matmul_mx(bank(("V", m, 0)), T.vq[:, lo:lo + 128], T.vs[:, lo:lo + 128], T.hq[:, lo:hi], T.hs[:, lo:hi],
                        True, True).then_inc(S["vv%d" % m], 1)

    k = 0
    for s in tk(STORES):
        lo, hi = int(s[0]), int(s[1])
        for m in range(lo, hi):
            y.wait_ge(S["yc%d" % m], 1)
        y.dma_start(T.y[:, EC * lo:EC * hi], T.yb[:, EC * lo:EC * hi]).then_inc(S.ydone, 16)
        k += 16
    y.wait_ge(S.ydone, k)
